import numpy as np
import ml_dtypes


def mxq(x, axis, fmt="e4m3"):
    dtype, down = {"e4m3": (ml_dtypes.float8_e4m3fn, 7), "e5m2": (ml_dtypes.float8_e5m2, 14)}[fmt]
    v = np.moveaxis(np.asarray(x, np.float32).astype(ml_dtypes.bfloat16).astype(np.float64), axis, -1)
    blocks = v.reshape(v.shape[:-1] + (-1, 32))
    amax = np.abs(blocks).max(-1, keepdims=True)
    byte = np.maximum(np.where(amax > 0, np.frexp(amax)[1] - 1 + 127, 0) - down, 1)
    scale = np.exp2(byte - 127.0)
    codes = (blocks / scale).astype(np.float32).astype(dtype).astype(np.float64)
    return np.moveaxis((codes * scale).reshape(v.shape), -1, axis)


WIDE = False


def mx_kscale(k):
    if not WIDE:
        return np.ones(k)
    levels = np.array([10, -10, 5, -5, 0])
    if k % 512:
        return np.exp2(np.random.permutation(np.resize(levels, k // 32))).repeat(32)
    a = np.empty((k // 512, 16))
    for p in range(k // 512):
        a[p, :8] = np.random.permutation(np.resize(levels, 8))
        for g in range(8):
            far = levels[np.abs(levels - a[p, g]) >= 10]
            a[p, g + 8] = far[np.random.randint(len(far))]
    return np.exp2(a.ravel()).repeat(32)


def f64(x):
    return np.asarray(x).astype(np.float64)


def striped(idx):
    return np.tile(idx.reshape(-1, 16).T, (8, 1)).astype(np.uint16)


def unstriped(offs):
    return offs[:16].T.reshape(-1).astype(np.int64)


def striped8(idx):
    return np.concatenate([x.reshape(-1, 16).T for x in idx]).astype(np.uint16)


def runs(offs, k):
    lists = np.stack([offs[16 * r : 16 * r + 16].T.reshape(-1) for r in range(8)]).astype(np.int64)
    return lists[np.arange(k) % 512 // 64]


def pack_weight(w):
    k, n = w.shape
    w = f64(np.asarray(w, np.float32).astype(ml_dtypes.bfloat16)).reshape(k // 32, 32, n)
    amax = np.abs(w).max(1)
    byte = np.clip(np.where(amax > 0, np.frexp(amax)[1] - 1 + 127 - 7, 1), 1, 254)
    scaled = (w * np.exp2(127.0 - byte)[:, None, :]).reshape(k, n).astype(np.float32)
    words = np.ascontiguousarray(scaled.reshape(k // 512, 128, 4, n).transpose(0, 1, 3, 2)).astype(ml_dtypes.float8_e4m3fn).view(np.uint8)
    return words, np.ascontiguousarray(byte.astype(np.uint8).reshape(k // 512, 16, n))


def unpack_weight(words, scales):
    g, p, n, _ = words.shape
    vals = np.ascontiguousarray(words).view(ml_dtypes.float8_e4m3fn).astype(np.float64) * np.repeat(np.exp2(scales.astype(np.float64) - 127.0), 8, axis=1)[..., None]
    return vals.transpose(0, 1, 3, 2).reshape(g * 512, n)


def sigmoid(v):
    return 1.0 / (1.0 + np.exp(-np.maximum(v, -700.0)))

def planes(y):
    n, m = y.shape
    v = y.astype(np.float32).astype(ml_dtypes.bfloat16).astype(np.float64).reshape(n // 32, 32, m)
    top = np.abs(v).max(1)
    byte = np.clip(np.where(top > 0, np.frexp(top)[1] - 1 + 127 - 7, 1), 1, 254)
    codes = (v * np.exp2(127.0 - byte)[:, None, :]).reshape(n, m).astype(np.float32).astype(ml_dtypes.float8_e4m3fn).view(np.uint8)
    words = codes.reshape(n // 512, 128, 4, m).transpose(0, 1, 3, 2)
    return np.ascontiguousarray(words), np.ascontiguousarray(byte.astype(np.uint8).reshape(n // 512, 16, m))


K, T, S, N, G, H = 512, 2048, 512, 512, 2048, 512


def setup_inputs():
    n = np.random.standard_normal
    s = mx_kscale(K)[:, None]
    u = mx_kscale(S)
    packed_xT = pack_weight(n((K, T)) * s)
    packed_dT = pack_weight(n((K, G)) / s)
    packed_w1 = pack_weight(n((H, N)) / np.sqrt(H) / u[:, None])
    return {
        "x_words": packed_xT[0],
        "x_scales": packed_xT[1],
        "d_words": packed_dT[0],
        "d_scales": packed_dT[1],
        "gn": (np.random.uniform(0.5, 1.5, (H, 1)) * u[:, None]).astype(np.float32),
        "w1_words": packed_w1[0],
        "w1_scales": packed_w1[1],
        "offs": striped8(np.random.randint(0, T, (8, S))),
        "k1": striped8(np.random.randint(0, G, (8, H))),
        "n1": striped(np.random.permutation(S)),
        "n2": striped(np.random.permutation(S)),
        "n3": striped(np.random.permutation(S)),
        "n4": striped(np.random.permutation(S)),
    }


def reference(x_words, x_scales, d_words, d_scales, gn, w1_words, w1_scales, offs, k1, n1, n2, n3, n4):
    d_k1 = unpack_weight(d_words, d_scales)[np.arange(K)[:, None], runs(k1, K)]
    xq = unpack_weight(x_words, x_scales)[np.arange(K)[:, None], runs(offs, K)]
    h = 0.0625 * (d_k1.T @ xq)
    z = f64(gn) * (h + (sigmoid(h[:, unstriped(n1)])) * (h[:, unstriped(n2)] - h))
    h2 = unpack_weight(w1_words, w1_scales).T @ mxq(z, 0, "e4m3")
    out_0 = 0.75 * (h2[:, unstriped(n3)] + h2[:, unstriped(n4)]) - h2
    return (out_0,) + planes(out_0)

@@ -1,0 +1,224 @@
+from contextlib import ExitStack
+
+import concourse.mybir as mybir
+
+F32 = mybir.dt.float32
+BF16 = mybir.dt.bfloat16
+I32 = mybir.dt.int32
+U32 = mybir.dt.uint32
+U16 = mybir.dt.uint16
+U8 = mybir.dt.uint8
+FP8X4 = mybir.dt.float8_e4m3fn_x4
+ALU = mybir.AluOpType
+ACT = mybir.ActivationFunctionType
+
+P = 128
+PACK = 4
+TABLE = 2048
+S = 512
+FLOPS = 2 * 2 * 512 * 512 * 512
+
+HALF = S // 2
+
+
+def half(c):
+    return slice(c * HALF, (c + 1) * HALF)
+
+
+def entries(offsets, c):
+    return offsets[:, c * HALF // 16 : (c + 1) * HALF // 16]
+
+
+def tile_picked_hpqtracklap_none_po_kernel(
+    tc, x_words, x_scales, d_words, d_scales, gn, w1_words, w1_scales, offs, k1, n1, n2, n3, n4, out_0, out_1, out_2
+):
+    nc = tc.nc
+    with ExitStack() as ctx:
+        lists = ctx.enter_context(tc.tile_pool(name="lists", bufs=1))
+        keep = ctx.enter_context(tc.tile_pool(name="keep", bufs=1))
+        psum = ctx.enter_context(tc.psum_pool(name="psum", bufs=1))
+
+        def load_list(name, src):
+            tile = lists.tile([P, S // 16], U16, name=name)
+            nc.sync.dma_start(tile[:], src)
+            return tile
+
+        def load_scale_window(name, scales, width):
+            tile = keep.tile([P, width], U8, name=name, align_bytes=64)
+            rows = scales[0].bitcast(I32)
+            nc.sync.dma_start(tile[:].bitcast(I32), rows.unsqueeze(1).to_broadcast([16, 8, width // 4]))
+            return tile
+
+        def load_words(name, words, width, tag):
+            tile = keep.tile([P, width], I32, name=name, tag=tag, align_bytes=64)
+            nc.sync.dma_start(tile[:], words[0].rearrange("p n t -> p (n t)").bitcast(I32))
+            return tile
+
+        k1_t = load_list("k1_t", k1)
+        ds_win = load_scale_window("ds_win", d_scales, TABLE)
+        offs_t = load_list("offs_t", offs)
+        xs_win = load_scale_window("xs_win", x_scales, TABLE)
+        ws_raw = load_scale_window("ws_raw", w1_scales, S)
+        gain = keep.tile([P, PACK], F32)
+        nc.sync.dma_start(gain[:], gn.rearrange("(p t) o -> p (t o)", t=PACK))
+        dw_win = load_words("dw_win", d_words, TABLE, "dw_win")
+        xw_win = load_words("xw_win", x_words, TABLE, "xw_win")
+        n2_t = load_list("n2_t", n2)
+        n1_t = load_list("n1_t", n1)
+        n3_t = load_list("n3_t", n3)
+        n4_t = load_list("n4_t", n4)
+
+
+        def deal_words(copy, dst, src):
+            copy(
+                dst.rearrange("p (t c i) -> p c t i", t=PACK, i=4),
+                src.rearrange("p (c i t) -> p c t i", t=PACK, i=4),
+            )
+
+        def deal_bytes(dst, src):
+            nc.vector.tensor_copy(
+                dst.rearrange("p (t c i) -> p c t i", t=PACK, i=16),
+                src.rearrange("p (c i t) -> p c t i", t=PACK, i=16),
+            )
+
+        planes = keep.tile([P, 3 * S], U8, align_bytes=64)
+        ds_pick = keep.tile([P, S], U8, align_bytes=64)
+        nc.vector.tensor_copy(ds_pick[:], ds_win[:].indirect(k1_t[:]))
+        deal_bytes(planes[:, :S], ds_pick[:])
+        deal_bytes(planes[:, 2 * S :], ws_raw[:])
+        xs_pick = keep.tile([P, S], U8, align_bytes=64)
+        nc.vector.tensor_copy(xs_pick[:], xs_win[:].indirect(offs_t[:]))
+        nc.vector.tensor_copy(planes[:, S : 2 * S].bitcast(I32), xs_pick[:].bitcast(I32))
+        for j in range(1, 4):
+            nc.scalar.dma_start(planes[j:P:32, :].bitcast(I32), planes[8 * j : P : 32, :].bitcast(I32))
+
+        dw_pick = keep.tile([P, S], U32, align_bytes=64)
+        nc.vector.tensor_copy(dw_pick[:], dw_win[:].bitcast(U32).indirect(k1_t[:]))
+        dw_dealt = keep.tile([P, S], I32, align_bytes=64)
+        deal_words(nc.vector.tensor_copy, dw_dealt[:], dw_pick[:].bitcast(I32))
+
+        ww_raw = load_words("ww_raw", w1_words, S, "dw_win")
+        gain16 = keep.tile([P, PACK], F32)
+        nc.vector.tensor_scalar(gain16[:], gain[:], 0.0625, None, ALU.mult)
+
+        xw_pick = [keep.tile([P, HALF], U32, name=f"xw_pick{c}", align_bytes=64) for c in range(2)]
+        for c in range(2):
+            nc.vector.tensor_copy(xw_pick[c][:], xw_win[:].bitcast(U32).indirect(entries(offs_t, c)))
+
+        hg = keep.tile([P, PACK, S], F32)
+        sg = [keep.tile([P, S], F32, name=f"sg{t}") for t in range(PACK)]
+        h_ps = {}
+
+        def first_product(t, c):
+            rows = slice(t * P, (t + 1) * P)
+            h_ps[t, c] = psum.tile([P, HALF], F32, name=f"h_ps{t}{c}", tag=f"bank{t}{c}")
+            nc.tensor.matmul_mx(
+                out=h_ps[t, c][:],
+                lhsT=dw_dealt[:, rows].bitcast(FP8X4),
+                lhsT_scale=planes[:, rows],
+                rhs=xw_pick[c][:].bitcast(FP8X4),
+                rhs_scale=planes[:, S + c * HALF : S + (c + 1) * HALF],
+                start=True,
+                stop=True,
+            )
+
+        for pair in range(2):
+            for c in range(2):
+                for t in (2 * pair, 2 * pair + 1):
+                    first_product(t, c)
+
+        def scale_h(t):
+            for c in range(2):
+                if t < 2:
+                    nc.vector.tensor_scalar(hg[:, t, half(c)], h_ps[t, c][:], gain16[:, t : t + 1], None, ALU.mult)
+                else:
+                    nc.scalar.activation(hg[:, t, half(c)], h_ps[t, c][:], ACT.Copy, scale=gain16[:, t : t + 1])
+
+        def gate_h(t):
+            for c in range(2):
+                nc.scalar.activation(sg[t][:, half(c)], h_ps[t, c][:], ACT.Sigmoid, scale=0.0625)
+
+        far = [keep.tile([P, PACK, HALF], F32, name=f"far{c}") for c in range(2)]
+        diff = [keep.tile([P, PACK, HALF], F32, name=f"diff{c}") for c in range(2)]
+        move = [keep.tile([P, PACK, HALF], F32, name=f"move{c}") for c in range(2)]
+        h2 = [keep.tile([P, S], F32, name=f"h2_{t}") for t in range(PACK)]
+        ww_dealt = keep.tile([P, S], U32, align_bytes=64)
+
+        def blend(t, c):
+            nc.scalar.activation(far[c][:, t, :], hg[:, t, :].indirect(entries(n2_t, c)), ACT.Copy)
+            nc.vector.tensor_tensor(diff[c][:, t, :], far[c][:, t, :], hg[:, t, half(c)], ALU.subtract)
+            nc.vector.tensor_tensor(move[c][:, t, :], sg[t][:].indirect(entries(n1_t, c)), diff[c][:, t, :], ALU.mult)
+
+        def second_product(c):
+            z = keep.tile([P, HALF, PACK], BF16, name=f"z{c}", align_bytes=64)
+            nc.vector.tensor_tensor(
+                z[:].rearrange("p (c i) t -> p c t i", i=4),
+                move[c][:].rearrange("p t (c i) -> p c t i", i=4),
+                hg[:, :, half(c)].rearrange("p t (c i) -> p c t i", i=4),
+                ALU.add,
+            )
+            z_codes = keep.tile([P, HALF], U32, name=f"z_codes{c}", align_bytes=64)
+            z_scales = keep.tile([P, HALF], U8, name=f"z_scales{c}", align_bytes=64)
+            nc.vector.quantize_mx(out=z_codes[:].bitcast(FP8X4), scales=z_scales[:], in_=z[:].rearrange("p c t -> p (c t)"))
+            for t in range(PACK):
+                acc = psum.tile([P, HALF], F32, name=f"h2_ps{t}{c}", tag=f"bank{t}{c}")
+                nc.tensor.matmul_mx(
+                    out=acc[:],
+                    lhsT=ww_dealt[:, t * P : (t + 1) * P].bitcast(FP8X4),
+                    lhsT_scale=planes[:, 2 * S + t * P : 2 * S + (t + 1) * P],
+                    rhs=z_codes[:].bitcast(FP8X4),
+                    rhs_scale=z_scales[:],
+                    start=True,
+                    stop=True,
+                )
+                copy = nc.vector.tensor_copy if (t, c) == (0, 1) else nc.scalar.copy
+                copy(h2[t][:, half(c)], acc[:])
+
+        for t in range(2):
+            gate_h(t)
+            scale_h(t)
+        for t in range(2):
+            for c in range(2):
+                blend(t, c)
+        for t in range(2, PACK):
+            scale_h(t)
+            gate_h(t)
+            blend(t, 0)
+        deal_words(nc.scalar.copy, ww_dealt[:], ww_raw[:].bitcast(U32))
+        second_product(0)
+        for t in range(2, PACK):
+            blend(t, 1)
+        second_product(1)
+
+        out_rows = out_0.rearrange("(p t) j -> p t j", t=PACK)
+        out_words = out_1[0].rearrange("p n t -> p (n t)").bitcast(I32)
+        y_scales = keep.tile([P, S], U8, align_bytes=64)
+        for c in range(2):
+            near = keep.tile([P, PACK, HALF], F32, name=f"near{c}")
+            both = keep.tile([P, PACK, HALF], F32, name=f"both{c}")
+            y = keep.tile([P, PACK, HALF], F32, name=f"y{c}")
+            for t in range(PACK):
+                window = h2[t][:].indirect(entries(n3_t, c))
+                if (t, c) == (0, 0):
+                    nc.vector.tensor_copy(near[:, t, :], window)
+                else:
+                    nc.scalar.activation(near[:, t, :], window, ACT.Copy)
+                nc.vector.tensor_tensor(both[:, t, :], h2[t][:].indirect(entries(n4_t, c)), near[:, t, :], ALU.add)
+                nc.vector.scalar_tensor_tensor(
+                    y[:, t, :], both[:, t, :], 0.75, h2[t][:, half(c)], ALU.mult, ALU.subtract
+                )
+                if c == 1:
+                    nc.sync.dma_start(out_rows[:, t, half(c)], y[:, t, :])
+            if c == 0:
+                nc.sync.dma_start(out_rows[:, :, half(c)], y[:])
+            y_bf = keep.tile([P, HALF, PACK], BF16, name=f"y_bf{c}", align_bytes=64)
+            copy = nc.vector.tensor_copy if c == 1 else nc.scalar.copy
+            copy(y_bf[:].rearrange("p (c i) t -> p c t i", i=4), y[:].rearrange("p t (c i) -> p c t i", i=4))
+            y_codes = keep.tile([P, HALF], I32, name=f"y_codes{c}", align_bytes=64)
+            nc.vector.quantize_mx(
+                out=y_codes[:].bitcast(FP8X4), scales=y_scales[:, half(c)], in_=y_bf[:].rearrange("p c t -> p (c t)")
+            )
+            nc.sync.dma_start(out_words[:, half(c)], y_codes[:])
+        for q in range(4):
+            queue = nc.sync if q == 3 else nc.scalar
+            queue.dma_start(out_2[0, 4 * q : 4 * q + 4, :].bitcast(I32), y_scales[32 * q : 32 * q + 4, :].bitcast(I32))

@@ -54,19 +54,22 @@ def tile_picked_hpqtracklap_none_po_kernel(
             nc.sync.dma_start(tile[:], words[0].rearrange("p n t -> p (n t)").bitcast(I32))
             return tile
 
-        k1_t = load_list("k1_t", k1)
         ds_win = load_scale_window("ds_win", d_scales, TABLE)
+        k1_t = load_list("k1_t", k1)
         offs_t = load_list("offs_t", offs)
         xs_win = load_scale_window("xs_win", x_scales, TABLE)
-        ws_raw = load_scale_window("ws_raw", w1_scales, S)
-        gain = keep.tile([P, PACK], F32)
-        nc.sync.dma_start(gain[:], gn.rearrange("(p t) o -> p (t o)", t=PACK))
         dw_win = load_words("dw_win", d_words, TABLE, "dw_win")
-        xw_win = load_words("xw_win", x_words, TABLE, "xw_win")
         n2_t = load_list("n2_t", n2)
         n1_t = load_list("n1_t", n1)
+        xw_win = load_words("xw_win", x_words, TABLE, "xw_win")
         n3_t = load_list("n3_t", n3)
         n4_t = load_list("n4_t", n4)
+        ww_raw = load_words("ww_raw", w1_words, S, "ww_raw")
+        ws_raw = load_scale_window("ws_raw", w1_scales, S)
+        gain = keep.tile([P, PACK], F32)
+        nc.gpsimd.dma_start(gain[:], gn.rearrange("(p t) o -> p (t o)", t=PACK))
+        gain16 = keep.tile([P, PACK], F32)
+        nc.gpsimd.tensor_scalar(gain16[:], gain[:], 0.0625, 0.0, ALU.mult, ALU.add)
 
 
         def deal_words(copy, dst, src):
@@ -81,29 +84,34 @@ def tile_picked_hpqtracklap_none_po_kernel(
                 src.rearrange("p (c i t) -> p c t i", t=PACK, i=16),
             )
 
-        planes = keep.tile([P, 3 * S], U8, align_bytes=64)
+        def gather_rows(queue, plane):
+            for j in range(1, 4):
+                queue.dma_start(plane[j:P:32, :].bitcast(I32), plane[8 * j : P : 32, :].bitcast(I32))
+
+        planes = keep.tile([P, 2 * S], U8, align_bytes=64)
         ds_pick = keep.tile([P, S], U8, align_bytes=64)
         nc.vector.tensor_copy(ds_pick[:], ds_win[:].indirect(k1_t[:]))
         deal_bytes(planes[:, :S], ds_pick[:])
-        deal_bytes(planes[:, 2 * S :], ws_raw[:])
         xs_pick = keep.tile([P, S], U8, align_bytes=64)
         nc.vector.tensor_copy(xs_pick[:], xs_win[:].indirect(offs_t[:]))
         nc.vector.tensor_copy(planes[:, S : 2 * S].bitcast(I32), xs_pick[:].bitcast(I32))
-        for j in range(1, 4):
-            nc.scalar.dma_start(planes[j:P:32, :].bitcast(I32), planes[8 * j : P : 32, :].bitcast(I32))
+        gather_rows(nc.scalar, planes)
 
         dw_pick = keep.tile([P, S], U32, align_bytes=64)
         nc.vector.tensor_copy(dw_pick[:], dw_win[:].bitcast(U32).indirect(k1_t[:]))
         dw_dealt = keep.tile([P, S], I32, align_bytes=64)
         deal_words(nc.vector.tensor_copy, dw_dealt[:], dw_pick[:].bitcast(I32))
 
-        ww_raw = load_words("ww_raw", w1_words, S, "dw_win")
-        gain16 = keep.tile([P, PACK], F32)
-        nc.vector.tensor_scalar(gain16[:], gain[:], 0.0625, None, ALU.mult)
+        ww_dealt = keep.tile([P, S], I32, align_bytes=64)
+        deal_words(nc.gpsimd.tensor_copy, ww_dealt[:], ww_raw[:])
 
         xw_pick = [keep.tile([P, HALF], U32, name=f"xw_pick{c}", align_bytes=64) for c in range(2)]
         for c in range(2):
             nc.vector.tensor_copy(xw_pick[c][:], xw_win[:].bitcast(U32).indirect(entries(offs_t, c)))
+
+        ws_plane = keep.tile([P, S], U8, align_bytes=64)
+        deal_bytes(ws_plane[:], ws_raw[:])
+        gather_rows(nc.sync, ws_plane)
 
         hg = keep.tile([P, PACK, S], F32)
         sg = [keep.tile([P, S], F32, name=f"sg{t}") for t in range(PACK)]
@@ -127,98 +135,174 @@ def tile_picked_hpqtracklap_none_po_kernel(
                 for t in (2 * pair, 2 * pair + 1):
                     first_product(t, c)
 
-        def scale_h(t):
-            for c in range(2):
-                if t < 2:
-                    nc.vector.tensor_scalar(hg[:, t, half(c)], h_ps[t, c][:], gain16[:, t : t + 1], None, ALU.mult)
-                else:
-                    nc.scalar.activation(hg[:, t, half(c)], h_ps[t, c][:], ACT.Copy, scale=gain16[:, t : t + 1])
+        def scale_h(t, c):
+            if t < 2:
+                nc.vector.tensor_scalar(hg[:, t, half(c)], h_ps[t, c][:], gain16[:, t : t + 1], None, ALU.mult)
+            else:
+                nc.scalar.activation(hg[:, t, half(c)], h_ps[t, c][:], ACT.Copy, scale=gain16[:, t : t + 1])
 
-        def gate_h(t):
-            for c in range(2):
-                nc.scalar.activation(sg[t][:, half(c)], h_ps[t, c][:], ACT.Sigmoid, scale=0.0625)
+        def gate_h(t, c):
+            nc.scalar.activation(sg[t][:, half(c)], h_ps[t, c][:], ACT.Sigmoid, scale=0.0625)
 
         far = [keep.tile([P, PACK, HALF], F32, name=f"far{c}") for c in range(2)]
         diff = [keep.tile([P, PACK, HALF], F32, name=f"diff{c}") for c in range(2)]
         move = [keep.tile([P, PACK, HALF], F32, name=f"move{c}") for c in range(2)]
+        gate = keep.tile([P, 2, HALF], F32)
         h2 = [keep.tile([P, S], F32, name=f"h2_{t}") for t in range(PACK)]
-        ww_dealt = keep.tile([P, S], U32, align_bytes=64)
 
-        def blend(t, c):
-            nc.scalar.activation(far[c][:, t, :], hg[:, t, :].indirect(entries(n2_t, c)), ACT.Copy)
+        def fetch_far(t, c):
+            window = hg[:, t, :].indirect(entries(n2_t, c))
+            if (t, c) == (0, 0):
+                nc.vector.tensor_copy(far[c][:, t, :], window)
+            else:
+                nc.scalar.activation(far[c][:, t, :], window, ACT.Copy)
+
+        def make_diff(t, c):
             nc.vector.tensor_tensor(diff[c][:, t, :], far[c][:, t, :], hg[:, t, half(c)], ALU.subtract)
-            nc.vector.tensor_tensor(move[c][:, t, :], sg[t][:].indirect(entries(n1_t, c)), diff[c][:, t, :], ALU.mult)
 
-        def second_product(c):
-            z = keep.tile([P, HALF, PACK], BF16, name=f"z{c}", align_bytes=64)
+        def make_move(t, c):
+            window = sg[t][:].indirect(entries(n1_t, c))
+            if c == 1 and t >= 2:
+                nc.scalar.activation(gate[:, t - 2, :], window, ACT.Copy)
+                nc.vector.tensor_tensor(move[c][:, t, :], gate[:, t - 2, :], diff[c][:, t, :], ALU.mult)
+            else:
+                nc.vector.tensor_tensor(move[c][:, t, :], window, diff[c][:, t, :], ALU.mult)
+
+        def make_z(a, w):
+            c, lo = divmod(a, HALF)
+            z = keep.tile([P, w, PACK], BF16, name=f"z{a}", align_bytes=64)
             nc.vector.tensor_tensor(
                 z[:].rearrange("p (c i) t -> p c t i", i=4),
-                move[c][:].rearrange("p t (c i) -> p c t i", i=4),
-                hg[:, :, half(c)].rearrange("p t (c i) -> p c t i", i=4),
+                move[c][:, :, lo : lo + w].rearrange("p t (c i) -> p c t i", i=4),
+                hg[:, :, a : a + w].rearrange("p t (c i) -> p c t i", i=4),
                 ALU.add,
             )
-            z_codes = keep.tile([P, HALF], U32, name=f"z_codes{c}", align_bytes=64)
-            z_scales = keep.tile([P, HALF], U8, name=f"z_scales{c}", align_bytes=64)
-            nc.vector.quantize_mx(out=z_codes[:].bitcast(FP8X4), scales=z_scales[:], in_=z[:].rearrange("p c t -> p (c t)"))
-            for t in range(PACK):
-                acc = psum.tile([P, HALF], F32, name=f"h2_ps{t}{c}", tag=f"bank{t}{c}")
-                nc.tensor.matmul_mx(
-                    out=acc[:],
-                    lhsT=ww_dealt[:, t * P : (t + 1) * P].bitcast(FP8X4),
-                    lhsT_scale=planes[:, 2 * S + t * P : 2 * S + (t + 1) * P],
-                    rhs=z_codes[:].bitcast(FP8X4),
-                    rhs_scale=z_scales[:],
-                    start=True,
-                    stop=True,
-                )
-                copy = nc.vector.tensor_copy if (t, c) == (0, 1) else nc.scalar.copy
-                copy(h2[t][:, half(c)], acc[:])
+            return z
 
-        for t in range(2):
-            gate_h(t)
-            scale_h(t)
-        for t in range(2):
-            for c in range(2):
-                blend(t, c)
-        for t in range(2, PACK):
-            scale_h(t)
-            gate_h(t)
-            blend(t, 0)
-        deal_words(nc.scalar.copy, ww_dealt[:], ww_raw[:].bitcast(U32))
-        second_product(0)
-        for t in range(2, PACK):
-            blend(t, 1)
-        second_product(1)
+        def quantize_z(z, a, w):
+            z_codes = keep.tile([P, w], U32, name=f"z_codes{a}", align_bytes=64)
+            z_scales = keep.tile([P, w], U8, name=f"z_scales{a}", align_bytes=64)
+            nc.vector.quantize_mx(out=z_codes[:].bitcast(FP8X4), scales=z_scales[:], in_=z[:].rearrange("p c t -> p (c t)"))
+            return z_codes, z_scales
+
+        def second_product(operand, t, a, w, bank):
+            acc = psum.tile([P, w], F32, name=f"h2_ps{t}_{a}", tag=f"bank{t}{bank}")
+            nc.tensor.matmul_mx(
+                out=acc[:],
+                lhsT=ww_dealt[:, t * P : (t + 1) * P].bitcast(FP8X4),
+                lhsT_scale=ws_plane[:, t * P : (t + 1) * P],
+                rhs=operand[0][:].bitcast(FP8X4),
+                rhs_scale=operand[1][:],
+                start=True,
+                stop=True,
+            )
+            return acc
+
+        gate_h(0, 0)
+        scale_h(0, 0)
+        gate_h(1, 0)
+        scale_h(0, 1)
+        gate_h(0, 1)
+        scale_h(1, 0)
+        fetch_far(0, 1)
+        fetch_far(0, 0)
+        scale_h(1, 1)
+        gate_h(1, 1)
+        make_diff(0, 0)
+        items = [(0, 0), (0, 1), (1, 0), (1, 1), (2, 0), (3, 0), (2, 1), (3, 1)]
+        for before, (t, c) in zip(items, items[1:]):
+            if t >= 2 and c == 0:
+                scale_h(t, 0)
+                scale_h(t, 1)
+            if t >= 1:
+                fetch_far(t, c)
+            if t >= 2 and c == 0:
+                gate_h(t, 0)
+                gate_h(t, 1)
+            make_diff(t, c)
+            if (t, c) == (3, 1):
+                z0 = make_z(0, HALF)
+            make_move(*before)
+        operand = quantize_z(z0, 0, HALF)
+        for t in range(PACK):
+            nc.scalar.copy(h2[t][:, half(0)], second_product(operand, t, 0, HALF, 0)[:])
+        make_move(3, 1)
+        QUARTER = HALF // 2
+        zs = [make_z(HALF + u * QUARTER, QUARTER) for u in range(2)]
+        operands = [quantize_z(zs[u], HALF + u * QUARTER, QUARTER) for u in range(2)]
+        accs = {}
+        for u in range(2):
+            for t in range(PACK):
+                accs[t, u] = second_product(operands[u], t, HALF + u * QUARTER, QUARTER, 1 - u)
+        for t in range(PACK):
+            nc.scalar.copy(h2[t][:, HALF : HALF + QUARTER], accs[t, 0][:])
 
         out_rows = out_0.rearrange("(p t) j -> p t j", t=PACK)
         out_words = out_1[0].rearrange("p n t -> p (n t)").bitcast(I32)
         y_scales = keep.tile([P, S], U8, align_bytes=64)
-        for c in range(2):
-            near = keep.tile([P, PACK, HALF], F32, name=f"near{c}")
-            both = keep.tile([P, PACK, HALF], F32, name=f"both{c}")
-            y = keep.tile([P, PACK, HALF], F32, name=f"y{c}")
-            for t in range(PACK):
-                window = h2[t][:].indirect(entries(n3_t, c))
-                if (t, c) == (0, 0):
-                    nc.vector.tensor_copy(near[:, t, :], window)
-                else:
-                    nc.scalar.activation(near[:, t, :], window, ACT.Copy)
-                nc.vector.tensor_tensor(both[:, t, :], h2[t][:].indirect(entries(n4_t, c)), near[:, t, :], ALU.add)
-                nc.vector.scalar_tensor_tensor(
-                    y[:, t, :], both[:, t, :], 0.75, h2[t][:, half(c)], ALU.mult, ALU.subtract
-                )
-                if c == 1:
-                    nc.sync.dma_start(out_rows[:, t, half(c)], y[:, t, :])
+        near = [keep.tile([P, PACK, HALF], F32, name=f"near{c}") for c in range(2)]
+        other = keep.tile([P, 2, HALF], F32)
+        both = [keep.tile([P, PACK, HALF], F32, name=f"both{c}") for c in range(2)]
+        y = [keep.tile([P, PACK, HALF], F32, name=f"y{c}") for c in range(2)]
+
+        def make_both(t, c):
             if c == 0:
-                nc.sync.dma_start(out_rows[:, :, half(c)], y[:])
-            y_bf = keep.tile([P, HALF, PACK], BF16, name=f"y_bf{c}", align_bytes=64)
-            copy = nc.vector.tensor_copy if c == 1 else nc.scalar.copy
-            copy(y_bf[:].rearrange("p (c i) t -> p c t i", i=4), y[:].rearrange("p t (c i) -> p c t i", i=4))
-            y_codes = keep.tile([P, HALF], I32, name=f"y_codes{c}", align_bytes=64)
-            nc.vector.quantize_mx(
-                out=y_codes[:].bitcast(FP8X4), scales=y_scales[:, half(c)], in_=y_bf[:].rearrange("p c t -> p (c t)")
+                copy = nc.vector.tensor_copy if t == 0 else nc.scalar.copy
+                copy(h2[t][:, HALF + QUARTER :], accs[t, 1][:])
+            window = h2[t][:].indirect(entries(n3_t, c))
+            if (t, c) == (0, 0):
+                nc.vector.tensor_copy(near[c][:, t, :], window)
+            else:
+                nc.scalar.activation(near[c][:, t, :], window, ACT.Copy)
+            window = h2[t][:].indirect(entries(n4_t, c))
+            if c == 1 and t >= 2:
+                nc.scalar.activation(other[:, t - 2, :], window, ACT.Copy)
+                nc.vector.tensor_tensor(both[c][:, t, :], other[:, t - 2, :], near[c][:, t, :], ALU.add)
+            else:
+                nc.vector.tensor_tensor(both[c][:, t, :], window, near[c][:, t, :], ALU.add)
+
+        def make_y(t, c):
+            nc.vector.scalar_tensor_tensor(
+                y[c][:, t, :], both[c][:, t, :], 0.75, h2[t][:, half(c)], ALU.mult, ALU.subtract
             )
-            nc.sync.dma_start(out_words[:, half(c)], y_codes[:])
+            if c == 1:
+                nc.sync.dma_start(out_rows[:, t, half(c)], y[c][:, t, :])
+
+        def round_y(copy, a, w):
+            c, lo = divmod(a, HALF)
+            y_bf = keep.tile([P, w, PACK], BF16, name=f"y_bf{a}", align_bytes=64)
+            copy(
+                y_bf[:].rearrange("p (c i) t -> p c t i", i=4),
+                y[c][:, :, lo : lo + w].rearrange("p t (c i) -> p c t i", i=4),
+            )
+            return y_bf
+
+        y_codes = [keep.tile([P, HALF], I32, name=f"y_codes{c}", align_bytes=64) for c in range(2)]
+
+        def quantize_y(y_bf, a, w):
+            c, lo = divmod(a, HALF)
+            nc.vector.quantize_mx(
+                out=y_codes[c][:, lo : lo + w].bitcast(FP8X4),
+                scales=y_scales[:, a : a + w],
+                in_=y_bf[:].rearrange("p c t -> p (c t)"),
+            )
+
+        items = [(t, c) for c in range(2) for t in range(PACK)]
+        make_both(0, 0)
+        for before, (t, c) in zip(items, items[1:]):
+            make_both(t, c)
+            make_y(*before)
+            if before == (3, 0):
+                nc.sync.dma_start(out_rows[:, :, half(0)], y[0][:])
+            if before == (1, 1):
+                y_bf0 = round_y(nc.scalar.copy, 0, HALF)
+        quantize_y(y_bf0, 0, HALF)
+        nc.sync.dma_start(out_words[:, half(0)], y_codes[0][:])
+        make_y(3, 1)
+        tails = [round_y(nc.vector.tensor_copy, HALF + u * QUARTER, QUARTER) for u in range(2)]
+        for u in range(2):
+            quantize_y(tails[u], HALF + u * QUARTER, QUARTER)
+        nc.sync.dma_start(out_words[:, half(1)], y_codes[1][:])
         for q in range(4):
             queue = nc.sync if q == 3 else nc.scalar
             queue.dma_start(out_2[0, 4 * q : 4 * q + 4, :].bitcast(I32), y_scales[32 * q : 32 * q + 4, :].bitcast(I32))

@@ -19,6 +19,8 @@ S = 512
 FLOPS = 2 * 2 * 512 * 512 * 512
 
 HALF = S // 2
+QUARTER = S // 4
+BIG = 3.0e38
 
 
 def half(c):
@@ -43,10 +45,10 @@ def tile_picked_hpqtracklap_none_po_kernel(
             nc.sync.dma_start(tile[:], src)
             return tile
 
-        def load_scale_window(name, scales, width):
+        def load_scale_window(queue, name, scales, width):
             tile = keep.tile([P, width], U8, name=name, align_bytes=64)
             rows = scales[0].bitcast(I32)
-            nc.sync.dma_start(tile[:].bitcast(I32), rows.unsqueeze(1).to_broadcast([16, 8, width // 4]))
+            queue.dma_start(tile[:].bitcast(I32), rows.unsqueeze(1).to_broadcast([16, 8, width // 4]))
             return tile
 
         def load_words(name, words, width, tag):
@@ -54,10 +56,10 @@ def tile_picked_hpqtracklap_none_po_kernel(
             nc.sync.dma_start(tile[:], words[0].rearrange("p n t -> p (n t)").bitcast(I32))
             return tile
 
-        ds_win = load_scale_window("ds_win", d_scales, TABLE)
+        ds_win = load_scale_window(nc.sync, "ds_win", d_scales, TABLE)
         k1_t = load_list("k1_t", k1)
         offs_t = load_list("offs_t", offs)
-        xs_win = load_scale_window("xs_win", x_scales, TABLE)
+        xs_win = load_scale_window(nc.sync, "xs_win", x_scales, TABLE)
         dw_win = load_words("dw_win", d_words, TABLE, "dw_win")
         n2_t = load_list("n2_t", n2)
         n1_t = load_list("n1_t", n1)
@@ -65,12 +67,9 @@ def tile_picked_hpqtracklap_none_po_kernel(
         n3_t = load_list("n3_t", n3)
         n4_t = load_list("n4_t", n4)
         ww_raw = load_words("ww_raw", w1_words, S, "ww_raw")
-        ws_raw = load_scale_window("ws_raw", w1_scales, S)
         gain = keep.tile([P, PACK], F32)
         nc.gpsimd.dma_start(gain[:], gn.rearrange("(p t) o -> p (t o)", t=PACK))
-        gain16 = keep.tile([P, PACK], F32)
-        nc.gpsimd.tensor_scalar(gain16[:], gain[:], 0.0625, 0.0, ALU.mult, ALU.add)
-
+        ws_raw = load_scale_window(nc.gpsimd, "ws_raw", w1_scales, S)
 
         def deal_words(copy, dst, src):
             copy(
@@ -78,8 +77,8 @@ def tile_picked_hpqtracklap_none_po_kernel(
                 src.rearrange("p (c i t) -> p c t i", t=PACK, i=4),
             )
 
-        def deal_bytes(dst, src):
-            nc.vector.tensor_copy(
+        def deal_bytes(copy, dst, src):
+            copy(
                 dst.rearrange("p (t c i) -> p c t i", t=PACK, i=16),
                 src.rearrange("p (c i t) -> p c t i", t=PACK, i=16),
             )
@@ -91,7 +90,7 @@ def tile_picked_hpqtracklap_none_po_kernel(
         planes = keep.tile([P, 2 * S], U8, align_bytes=64)
         ds_pick = keep.tile([P, S], U8, align_bytes=64)
         nc.vector.tensor_copy(ds_pick[:], ds_win[:].indirect(k1_t[:]))
-        deal_bytes(planes[:, :S], ds_pick[:])
+        deal_bytes(nc.vector.tensor_copy, planes[:, :S], ds_pick[:])
         xs_pick = keep.tile([P, S], U8, align_bytes=64)
         nc.vector.tensor_copy(xs_pick[:], xs_win[:].indirect(offs_t[:]))
         nc.vector.tensor_copy(planes[:, S : 2 * S].bitcast(I32), xs_pick[:].bitcast(I32))
@@ -99,9 +98,15 @@ def tile_picked_hpqtracklap_none_po_kernel(
 
         dw_pick = keep.tile([P, S], U32, align_bytes=64)
         nc.vector.tensor_copy(dw_pick[:], dw_win[:].bitcast(U32).indirect(k1_t[:]))
+        inverse = keep.tile([P, PACK], F32, tag="dw_win", align_bytes=64)
+        nc.vector.reciprocal(inverse[:], gain[:])
         dw_dealt = keep.tile([P, S], I32, align_bytes=64)
         deal_words(nc.vector.tensor_copy, dw_dealt[:], dw_pick[:].bitcast(I32))
 
+        gain16 = keep.tile([P, PACK], F32)
+        nc.gpsimd.tensor_scalar(gain16[:], gain[:], 0.0625, 0.0, ALU.mult, ALU.add)
+        ungain = keep.tile([P, PACK], F32)
+        nc.vector.tensor_scalar(ungain[:], inverse[:], -BIG, BIG, ALU.max, ALU.min)
         ww_dealt = keep.tile([P, S], I32, align_bytes=64)
         deal_words(nc.gpsimd.tensor_copy, ww_dealt[:], ww_raw[:])
 
@@ -109,12 +114,11 @@ def tile_picked_hpqtracklap_none_po_kernel(
         for c in range(2):
             nc.vector.tensor_copy(xw_pick[c][:], xw_win[:].bitcast(U32).indirect(entries(offs_t, c)))
 
-        ws_plane = keep.tile([P, S], U8, align_bytes=64)
-        deal_bytes(ws_plane[:], ws_raw[:])
+        ws_plane = keep.tile([P, S], U8, tag="ww_raw", align_bytes=64)
+        deal_bytes(nc.gpsimd.tensor_copy, ws_plane[:], ws_raw[:])
         gather_rows(nc.sync, ws_plane)
 
-        hg = keep.tile([P, PACK, S], F32)
-        sg = [keep.tile([P, S], F32, name=f"sg{t}") for t in range(PACK)]
+        hg = [keep.tile([P, S], F32, name=f"hg{t}") for t in range(PACK)]
         h_ps = {}
 
         def first_product(t, c):
@@ -130,52 +134,37 @@ def tile_picked_hpqtracklap_none_po_kernel(
                 stop=True,
             )
 
-        for pair in range(2):
-            for c in range(2):
-                for t in (2 * pair, 2 * pair + 1):
-                    first_product(t, c)
+        banks = [(0, 0), (1, 0), (0, 1), (1, 1), (2, 0), (2, 1), (3, 0), (3, 1)]
+        for t, c in banks:
+            first_product(t, c)
+        for t, c in banks:
+            nc.vector.tensor_scalar(hg[t][:, half(c)], h_ps[t, c][:], gain16[:, t : t + 1], None, ALU.mult)
 
-        def scale_h(t, c):
-            if t < 2:
-                nc.vector.tensor_scalar(hg[:, t, half(c)], h_ps[t, c][:], gain16[:, t : t + 1], None, ALU.mult)
-            else:
-                nc.scalar.activation(hg[:, t, half(c)], h_ps[t, c][:], ACT.Copy, scale=gain16[:, t : t + 1])
-
-        def gate_h(t, c):
-            nc.scalar.activation(sg[t][:, half(c)], h_ps[t, c][:], ACT.Sigmoid, scale=0.0625)
-
-        far = [keep.tile([P, PACK, HALF], F32, name=f"far{c}") for c in range(2)]
-        diff = [keep.tile([P, PACK, HALF], F32, name=f"diff{c}") for c in range(2)]
-        move = [keep.tile([P, PACK, HALF], F32, name=f"move{c}") for c in range(2)]
-        gate = keep.tile([P, 2, HALF], F32)
+        gate = [keep.tile([P, PACK, HALF], F32, name=f"gate{c}") for c in range(2)]
+        far = keep.tile([P, PACK, HALF], F32)
+        pull = [keep.tile([P, PACK, HALF], F32, name=f"pull{c}") for c in range(2)]
+        stay = [keep.tile([P, PACK, HALF], F32, name=f"stay{c}") for c in range(2)]
         h2 = [keep.tile([P, S], F32, name=f"h2_{t}") for t in range(PACK)]
 
-        def fetch_far(t, c):
-            window = hg[:, t, :].indirect(entries(n2_t, c))
-            if (t, c) == (0, 0):
-                nc.vector.tensor_copy(far[c][:, t, :], window)
+        def blend(t, c):
+            s_tc = gate[c][:, t, :]
+            nc.scalar.activation(s_tc, hg[t][:].indirect(entries(n1_t, c)), ACT.Sigmoid, scale=ungain[:, t : t + 1])
+            nc.vector.scalar_tensor_tensor(stay[c][:, t, :], s_tc, 1.0, hg[t][:, half(c)], ALU.subtract, ALU.mult)
+            window = hg[t][:].indirect(entries(n2_t, c))
+            if c == 0:
+                nc.vector.tensor_tensor(pull[c][:, t, :], window, s_tc, ALU.mult)
             else:
-                nc.scalar.activation(far[c][:, t, :], window, ACT.Copy)
-
-        def make_diff(t, c):
-            nc.vector.tensor_tensor(diff[c][:, t, :], far[c][:, t, :], hg[:, t, half(c)], ALU.subtract)
-
-        def make_move(t, c):
-            window = sg[t][:].indirect(entries(n1_t, c))
-            if c == 1 and t >= 2:
-                nc.scalar.activation(gate[:, t - 2, :], window, ACT.Copy)
-                nc.vector.tensor_tensor(move[c][:, t, :], gate[:, t - 2, :], diff[c][:, t, :], ALU.mult)
-            else:
-                nc.vector.tensor_tensor(move[c][:, t, :], window, diff[c][:, t, :], ALU.mult)
+                nc.scalar.activation(far[:, t, :], window, ACT.Copy)
+                nc.vector.tensor_tensor(pull[c][:, t, :], far[:, t, :], s_tc, ALU.mult)
 
         def make_z(a, w):
             c, lo = divmod(a, HALF)
             z = keep.tile([P, w, PACK], BF16, name=f"z{a}", align_bytes=64)
             nc.vector.tensor_tensor(
                 z[:].rearrange("p (c i) t -> p c t i", i=4),
-                move[c][:, :, lo : lo + w].rearrange("p t (c i) -> p c t i", i=4),
-                hg[:, :, a : a + w].rearrange("p t (c i) -> p c t i", i=4),
-                ALU.add,
+                pull[c][:, :, lo : lo + w].rearrange("p t (c i) -> p c t i", i=4),
+                stay[c][:, :, lo : lo + w].rearrange("p t (c i) -> p c t i", i=4),
+                ALU.subtract,
             )
             return z
 
@@ -198,44 +187,22 @@ def tile_picked_hpqtracklap_none_po_kernel(
             )
             return acc
 
-        gate_h(0, 0)
-        scale_h(0, 0)
-        gate_h(1, 0)
-        scale_h(0, 1)
-        gate_h(0, 1)
-        scale_h(1, 0)
-        fetch_far(0, 1)
-        fetch_far(0, 0)
-        scale_h(1, 1)
-        gate_h(1, 1)
-        make_diff(0, 0)
-        items = [(0, 0), (0, 1), (1, 0), (1, 1), (2, 0), (3, 0), (2, 1), (3, 1)]
-        for before, (t, c) in zip(items, items[1:]):
-            if t >= 2 and c == 0:
-                scale_h(t, 0)
-                scale_h(t, 1)
-            if t >= 1:
-                fetch_far(t, c)
-            if t >= 2 and c == 0:
-                gate_h(t, 0)
-                gate_h(t, 1)
-            make_diff(t, c)
-            if (t, c) == (3, 1):
-                z0 = make_z(0, HALF)
-            make_move(*before)
+        for t in range(PACK):
+            blend(t, 0)
+        blend(0, 1)
+        z0 = make_z(0, HALF)
+        blend(1, 1)
         operand = quantize_z(z0, 0, HALF)
+        blend(2, 1)
+        blend(3, 1)
         for t in range(PACK):
             nc.scalar.copy(h2[t][:, half(0)], second_product(operand, t, 0, HALF, 0)[:])
-        make_move(3, 1)
-        QUARTER = HALF // 2
         zs = [make_z(HALF + u * QUARTER, QUARTER) for u in range(2)]
         operands = [quantize_z(zs[u], HALF + u * QUARTER, QUARTER) for u in range(2)]
-        accs = {}
-        for u in range(2):
-            for t in range(PACK):
-                accs[t, u] = second_product(operands[u], t, HALF + u * QUARTER, QUARTER, 1 - u)
-        for t in range(PACK):
-            nc.scalar.copy(h2[t][:, HALF : HALF + QUARTER], accs[t, 0][:])
+        for t, u in banks:
+            a = HALF + u * QUARTER
+            copy = nc.scalar.copy if u == 0 and t < 2 else nc.vector.tensor_copy
+            copy(h2[t][:, a : a + QUARTER], second_product(operands[u], t, a, QUARTER, 1 - u)[:])
 
         out_rows = out_0.rearrange("(p t) j -> p t j", t=PACK)
         out_words = out_1[0].rearrange("p n t -> p (n t)").bitcast(I32)
@@ -246,14 +213,7 @@ def tile_picked_hpqtracklap_none_po_kernel(
         y = [keep.tile([P, PACK, HALF], F32, name=f"y{c}") for c in range(2)]
 
         def make_both(t, c):
-            if c == 0:
-                copy = nc.vector.tensor_copy if t == 0 else nc.scalar.copy
-                copy(h2[t][:, HALF + QUARTER :], accs[t, 1][:])
-            window = h2[t][:].indirect(entries(n3_t, c))
-            if (t, c) == (0, 0):
-                nc.vector.tensor_copy(near[c][:, t, :], window)
-            else:
-                nc.scalar.activation(near[c][:, t, :], window, ACT.Copy)
+            nc.scalar.activation(near[c][:, t, :], h2[t][:].indirect(entries(n3_t, c)), ACT.Copy)
             window = h2[t][:].indirect(entries(n4_t, c))
             if c == 1 and t >= 2:
                 nc.scalar.activation(other[:, t - 2, :], window, ACT.Copy)
@@ -294,11 +254,10 @@ def tile_picked_hpqtracklap_none_po_kernel(
             make_y(*before)
             if before == (3, 0):
                 nc.sync.dma_start(out_rows[:, :, half(0)], y[0][:])
-            if before == (1, 1):
-                y_bf0 = round_y(nc.scalar.copy, 0, HALF)
+        y_bf0 = round_y(nc.scalar.copy, 0, HALF)
+        make_y(3, 1)
         quantize_y(y_bf0, 0, HALF)
         nc.sync.dma_start(out_words[:, half(0)], y_codes[0][:])
-        make_y(3, 1)
         tails = [round_y(nc.vector.tensor_copy, HALF + u * QUARTER, QUARTER) for u in range(2)]
         for u in range(2):
             quantize_y(tails[u], HALF + u * QUARTER, QUARTER)

@@ -161,9 +161,9 @@ def tile_picked_hpqtracklap_none_po_kernel(
             c, lo = divmod(a, HALF)
             z = keep.tile([P, w, PACK], BF16, name=f"z{a}", align_bytes=64)
             nc.vector.tensor_tensor(
-                z[:].rearrange("p (c i) t -> p c t i", i=4),
-                pull[c][:, :, lo : lo + w].rearrange("p t (c i) -> p c t i", i=4),
-                stay[c][:, :, lo : lo + w].rearrange("p t (c i) -> p c t i", i=4),
+                z[:].rearrange("p (c i) t -> p c t i", i=2),
+                pull[c][:, :, lo : lo + w].rearrange("p t (c i) -> p c t i", i=2),
+                stay[c][:, :, lo : lo + w].rearrange("p t (c i) -> p c t i", i=2),
                 ALU.subtract,
             )
             return z
@@ -232,8 +232,8 @@ def tile_picked_hpqtracklap_none_po_kernel(
             c, lo = divmod(a, HALF)
             y_bf = keep.tile([P, w, PACK], BF16, name=f"y_bf{a}", align_bytes=64)
             copy(
-                y_bf[:].rearrange("p (c i) t -> p c t i", i=4),
-                y[c][:, :, lo : lo + w].rearrange("p t (c i) -> p c t i", i=4),
+                y_bf[:].rearrange("p (c i) t -> p c t i", i=2),
+                y[c][:, :, lo : lo + w].rearrange("p t (c i) -> p c t i", i=2),
             )
             return y_bf
 

from contextlib import ExitStack

import concourse.mybir as mybir

F32 = mybir.dt.float32
BF16 = mybir.dt.bfloat16
I32 = mybir.dt.int32
U32 = mybir.dt.uint32
U16 = mybir.dt.uint16
U8 = mybir.dt.uint8
FP8X4 = mybir.dt.float8_e4m3fn_x4
ALU = mybir.AluOpType
ACT = mybir.ActivationFunctionType

P = 128
PACK = 4
TABLE = 2048
S = 512
FLOPS = 2 * 2 * 512 * 512 * 512

HALF = S // 2
QUARTER = S // 4
BIG = 3.0e38


def half(c):
    return slice(c * HALF, (c + 1) * HALF)


def entries(offsets, c):
    return offsets[:, c * HALF // 16 : (c + 1) * HALF // 16]


def tile_picked_hpqtracklap_none_po_kernel(
    tc, x_words, x_scales, d_words, d_scales, gn, w1_words, w1_scales, offs, k1, n1, n2, n3, n4, out_0, out_1, out_2
):
    nc = tc.nc
    with ExitStack() as ctx:
        lists = ctx.enter_context(tc.tile_pool(name="lists", bufs=1))
        keep = ctx.enter_context(tc.tile_pool(name="keep", bufs=1))
        psum = ctx.enter_context(tc.psum_pool(name="psum", bufs=1))

        def load_list(name, src):
            tile = lists.tile([P, S // 16], U16, name=name)
            nc.sync.dma_start(tile[:], src)
            return tile

        def load_scale_window(queue, name, scales, width):
            tile = keep.tile([P, width], U8, name=name, align_bytes=64)
            rows = scales[0].bitcast(I32)
            queue.dma_start(tile[:].bitcast(I32), rows.unsqueeze(1).to_broadcast([16, 8, width // 4]))
            return tile

        def load_words(name, words, width, tag):
            tile = keep.tile([P, width], I32, name=name, tag=tag, align_bytes=64)
            nc.sync.dma_start(tile[:], words[0].rearrange("p n t -> p (n t)").bitcast(I32))
            return tile

        ds_win = load_scale_window(nc.sync, "ds_win", d_scales, TABLE)
        k1_t = load_list("k1_t", k1)
        offs_t = load_list("offs_t", offs)
        xs_win = load_scale_window(nc.sync, "xs_win", x_scales, TABLE)
        dw_win = load_words("dw_win", d_words, TABLE, "dw_win")
        n2_t = load_list("n2_t", n2)
        n1_t = load_list("n1_t", n1)
        xw_win = load_words("xw_win", x_words, TABLE, "xw_win")
        n3_t = load_list("n3_t", n3)
        n4_t = load_list("n4_t", n4)
        ww_raw = load_words("ww_raw", w1_words, S, "ww_raw")
        gain = keep.tile([P, PACK], F32)
        nc.gpsimd.dma_start(gain[:], gn.rearrange("(p t) o -> p (t o)", t=PACK))
        ws_raw = load_scale_window(nc.gpsimd, "ws_raw", w1_scales, S)

        def deal_words(copy, dst, src):
            copy(
                dst.rearrange("p (t c i) -> p c t i", t=PACK, i=4),
                src.rearrange("p (c i t) -> p c t i", t=PACK, i=4),
            )

        def deal_bytes(copy, dst, src):
            copy(
                dst.rearrange("p (t c i) -> p c t i", t=PACK, i=16),
                src.rearrange("p (c i t) -> p c t i", t=PACK, i=16),
            )

        def gather_rows(queue, plane):
            for j in range(1, 4):
                queue.dma_start(plane[j:P:32, :].bitcast(I32), plane[8 * j : P : 32, :].bitcast(I32))

        planes = keep.tile([P, 2 * S], U8, align_bytes=64)
        ds_pick = keep.tile([P, S], U8, align_bytes=64)
        nc.vector.tensor_copy(ds_pick[:], ds_win[:].indirect(k1_t[:]))
        deal_bytes(nc.vector.tensor_copy, planes[:, :S], ds_pick[:])
        xs_pick = keep.tile([P, S], U8, align_bytes=64)
        nc.vector.tensor_copy(xs_pick[:], xs_win[:].indirect(offs_t[:]))
        nc.vector.tensor_copy(planes[:, S : 2 * S].bitcast(I32), xs_pick[:].bitcast(I32))
        gather_rows(nc.scalar, planes)

        dw_pick = keep.tile([P, S], U32, align_bytes=64)
        nc.vector.tensor_copy(dw_pick[:], dw_win[:].bitcast(U32).indirect(k1_t[:]))
        inverse = keep.tile([P, PACK], F32, tag="dw_win", align_bytes=64)
        nc.vector.reciprocal(inverse[:], gain[:])
        dw_dealt = keep.tile([P, S], I32, align_bytes=64)
        deal_words(nc.vector.tensor_copy, dw_dealt[:], dw_pick[:].bitcast(I32))

        gain16 = keep.tile([P, PACK], F32)
        nc.gpsimd.tensor_scalar(gain16[:], gain[:], 0.0625, 0.0, ALU.mult, ALU.add)
        ungain = keep.tile([P, PACK], F32)
        nc.vector.tensor_scalar(ungain[:], inverse[:], -BIG, BIG, ALU.max, ALU.min)
        ww_dealt = keep.tile([P, S], I32, align_bytes=64)
        deal_words(nc.gpsimd.tensor_copy, ww_dealt[:], ww_raw[:])

        xw_pick = [keep.tile([P, HALF], U32, name=f"xw_pick{c}", align_bytes=64) for c in range(2)]
        for c in range(2):
            nc.vector.tensor_copy(xw_pick[c][:], xw_win[:].bitcast(U32).indirect(entries(offs_t, c)))

        ws_plane = keep.tile([P, S], U8, tag="ww_raw", align_bytes=64)
        deal_bytes(nc.gpsimd.tensor_copy, ws_plane[:], ws_raw[:])
        gather_rows(nc.sync, ws_plane)

        hg = [keep.tile([P, S], F32, name=f"hg{t}") for t in range(PACK)]
        h_ps = {}

        def first_product(t, c):
            rows = slice(t * P, (t + 1) * P)
            h_ps[t, c] = psum.tile([P, HALF], F32, name=f"h_ps{t}{c}", tag=f"bank{t}{c}")
            nc.tensor.matmul_mx(
                out=h_ps[t, c][:],
                lhsT=dw_dealt[:, rows].bitcast(FP8X4),
                lhsT_scale=planes[:, rows],
                rhs=xw_pick[c][:].bitcast(FP8X4),
                rhs_scale=planes[:, S + c * HALF : S + (c + 1) * HALF],
                start=True,
                stop=True,
            )

        banks = [(0, 0), (1, 0), (0, 1), (1, 1), (2, 0), (2, 1), (3, 0), (3, 1)]
        for t, c in banks:
            first_product(t, c)
        for t, c in banks:
            nc.vector.tensor_scalar(hg[t][:, half(c)], h_ps[t, c][:], gain16[:, t : t + 1], None, ALU.mult)

        gate = [keep.tile([P, PACK, HALF], F32, name=f"gate{c}") for c in range(2)]
        far = keep.tile([P, PACK, HALF], F32)
        pull = [keep.tile([P, PACK, HALF], F32, name=f"pull{c}") for c in range(2)]
        stay = [keep.tile([P, PACK, HALF], F32, name=f"stay{c}") for c in range(2)]
        h2 = [keep.tile([P, S], F32, name=f"h2_{t}") for t in range(PACK)]

        def blend(t, c):
            s_tc = gate[c][:, t, :]
            nc.scalar.activation(s_tc, hg[t][:].indirect(entries(n1_t, c)), ACT.Sigmoid, scale=ungain[:, t : t + 1])
            nc.vector.scalar_tensor_tensor(stay[c][:, t, :], s_tc, 1.0, hg[t][:, half(c)], ALU.subtract, ALU.mult)
            window = hg[t][:].indirect(entries(n2_t, c))
            if c == 0:
                nc.vector.tensor_tensor(pull[c][:, t, :], window, s_tc, ALU.mult)
            else:
                nc.scalar.activation(far[:, t, :], window, ACT.Copy)
                nc.vector.tensor_tensor(pull[c][:, t, :], far[:, t, :], s_tc, ALU.mult)

        def make_z(a, w):
            c, lo = divmod(a, HALF)
            z = keep.tile([P, w, PACK], BF16, name=f"z{a}", align_bytes=64)
            nc.vector.tensor_tensor(
                z[:].rearrange("p (c i) t -> p c t i", i=2),
                pull[c][:, :, lo : lo + w].rearrange("p t (c i) -> p c t i", i=2),
                stay[c][:, :, lo : lo + w].rearrange("p t (c i) -> p c t i", i=2),
                ALU.subtract,
            )
            return z

        def quantize_z(z, a, w):
            z_codes = keep.tile([P, w], U32, name=f"z_codes{a}", align_bytes=64)
            z_scales = keep.tile([P, w], U8, name=f"z_scales{a}", align_bytes=64)
            nc.vector.quantize_mx(out=z_codes[:].bitcast(FP8X4), scales=z_scales[:], in_=z[:].rearrange("p c t -> p (c t)"))
            return z_codes, z_scales

        def second_product(operand, t, a, w, bank):
            acc = psum.tile([P, w], F32, name=f"h2_ps{t}_{a}", tag=f"bank{t}{bank}")
            nc.tensor.matmul_mx(
                out=acc[:],
                lhsT=ww_dealt[:, t * P : (t + 1) * P].bitcast(FP8X4),
                lhsT_scale=ws_plane[:, t * P : (t + 1) * P],
                rhs=operand[0][:].bitcast(FP8X4),
                rhs_scale=operand[1][:],
                start=True,
                stop=True,
            )
            return acc

        for t in range(PACK):
            blend(t, 0)
        blend(0, 1)
        z0 = make_z(0, HALF)
        blend(1, 1)
        operand = quantize_z(z0, 0, HALF)
        blend(2, 1)
        blend(3, 1)
        for t in range(PACK):
            nc.scalar.copy(h2[t][:, half(0)], second_product(operand, t, 0, HALF, 0)[:])
        zs = [make_z(HALF + u * QUARTER, QUARTER) for u in range(2)]
        operands = [quantize_z(zs[u], HALF + u * QUARTER, QUARTER) for u in range(2)]
        for t, u in banks:
            a = HALF + u * QUARTER
            copy = nc.scalar.copy if u == 0 and t < 2 else nc.vector.tensor_copy
            copy(h2[t][:, a : a + QUARTER], second_product(operands[u], t, a, QUARTER, 1 - u)[:])

        out_rows = out_0.rearrange("(p t) j -> p t j", t=PACK)
        out_words = out_1[0].rearrange("p n t -> p (n t)").bitcast(I32)
        y_scales = keep.tile([P, S], U8, align_bytes=64)
        near = [keep.tile([P, PACK, HALF], F32, name=f"near{c}") for c in range(2)]
        other = keep.tile([P, 2, HALF], F32)
        both = [keep.tile([P, PACK, HALF], F32, name=f"both{c}") for c in range(2)]
        y = [keep.tile([P, PACK, HALF], F32, name=f"y{c}") for c in range(2)]

        def make_both(t, c):
            nc.scalar.activation(near[c][:, t, :], h2[t][:].indirect(entries(n3_t, c)), ACT.Copy)
            window = h2[t][:].indirect(entries(n4_t, c))
            if c == 1 and t >= 2:
                nc.scalar.activation(other[:, t - 2, :], window, ACT.Copy)
                nc.vector.tensor_tensor(both[c][:, t, :], other[:, t - 2, :], near[c][:, t, :], ALU.add)
            else:
                nc.vector.tensor_tensor(both[c][:, t, :], window, near[c][:, t, :], ALU.add)

        def make_y(t, c):
            nc.vector.scalar_tensor_tensor(
                y[c][:, t, :], both[c][:, t, :], 0.75, h2[t][:, half(c)], ALU.mult, ALU.subtract
            )
            if c == 1:
                nc.sync.dma_start(out_rows[:, t, half(c)], y[c][:, t, :])

        def round_y(copy, a, w):
            c, lo = divmod(a, HALF)
            y_bf = keep.tile([P, w, PACK], BF16, name=f"y_bf{a}", align_bytes=64)
            copy(
                y_bf[:].rearrange("p (c i) t -> p c t i", i=2),
                y[c][:, :, lo : lo + w].rearrange("p t (c i) -> p c t i", i=2),
            )
            return y_bf

        y_codes = [keep.tile([P, HALF], I32, name=f"y_codes{c}", align_bytes=64) for c in range(2)]

        def quantize_y(y_bf, a, w):
            c, lo = divmod(a, HALF)
            nc.vector.quantize_mx(
                out=y_codes[c][:, lo : lo + w].bitcast(FP8X4),
                scales=y_scales[:, a : a + w],
                in_=y_bf[:].rearrange("p c t -> p (c t)"),
            )

        items = [(t, c) for c in range(2) for t in range(PACK)]
        make_both(0, 0)
        for before, (t, c) in zip(items, items[1:]):
            make_both(t, c)
            make_y(*before)
            if before == (3, 0):
                nc.sync.dma_start(out_rows[:, :, half(0)], y[0][:])
        y_bf0 = round_y(nc.scalar.copy, 0, HALF)
        make_y(3, 1)
        quantize_y(y_bf0, 0, HALF)
        nc.sync.dma_start(out_words[:, half(0)], y_codes[0][:])
        tails = [round_y(nc.vector.tensor_copy, HALF + u * QUARTER, QUARTER) for u in range(2)]
        for u in range(2):
            quantize_y(tails[u], HALF + u * QUARTER, QUARTER)
        nc.sync.dma_start(out_words[:, half(1)], y_codes[1][:])
        for q in range(4):
            queue = nc.sync if q == 3 else nc.scalar
            queue.dma_start(out_2[0, 4 * q : 4 * q + 4, :].bitcast(I32), y_scales[32 * q : 32 * q + 4, :].bitcast(I32))
